import numpy as np
import ml_dtypes


def mxq(x, axis, fmt="e4m3"):
    dtype, down = {"e4m3": (ml_dtypes.float8_e4m3fn, 7), "e5m2": (ml_dtypes.float8_e5m2, 14)}[fmt]
    v = np.moveaxis(np.asarray(x, np.float32).astype(ml_dtypes.bfloat16).astype(np.float64), axis, -1)
    blocks = v.reshape(v.shape[:-1] + (-1, 32))
    amax = np.abs(blocks).max(-1, keepdims=True)
    byte = np.maximum(np.where(amax > 0, np.frexp(amax)[1] - 1 + 127, 0) - down, 1)
    scale = np.exp2(byte - 127.0)
    codes = (blocks / scale).astype(np.float32).astype(dtype).astype(np.float64)
    return np.moveaxis((codes * scale).reshape(v.shape), -1, axis)


WIDE = False


def mx_kscale(k):
    if not WIDE:
        return np.ones(k)
    levels = np.array([10, -10, 5, -5, 0])
    if k % 512:
        return np.exp2(np.random.permutation(np.resize(levels, k // 32))).repeat(32)
    a = np.empty((k // 512, 16))
    for p in range(k // 512):
        a[p, :8] = np.random.permutation(np.resize(levels, 8))
        for g in range(8):
            far = levels[np.abs(levels - a[p, g]) >= 10]
            a[p, g + 8] = far[np.random.randint(len(far))]
    return np.exp2(a.ravel()).repeat(32)


def f64(x):
    return np.asarray(x).astype(np.float64)


def striped(idx):
    return np.tile(idx.reshape(-1, 16).T, (8, 1)).astype(np.uint16)


def unstriped(offs):
    return offs[:16].T.reshape(-1).astype(np.int64)


E2M1 = np.array([0.0, 0.5, 1.0, 1.5, 2.0, 3.0, 4.0, 6.0, -0.0, -0.5, -1.0, -1.5, -2.0, -3.0, -4.0, -6.0])


def pack_weight(w, fmt):
    k, n = w.shape
    w = f64(np.asarray(w, np.float32).astype(ml_dtypes.bfloat16)).reshape(k // 32, 32, n)
    amax = np.abs(w).max(1)
    if fmt == "e4m3":
        byte = np.frexp(amax)[1] - 1 + 127 - 7
    else:
        mant, ex = np.frexp(amax / 6.0)
        byte = np.where(mant > 0.5, ex, ex - 1) + 127
    byte = np.clip(np.where(amax > 0, byte, 1), 1, 254)
    scaled = (w * np.exp2(127.0 - byte)[:, None, :]).reshape(k, n).astype(np.float32)
    by_word = np.ascontiguousarray(scaled.reshape(k // 512, 128, 4, n).transpose(0, 1, 3, 2))
    if fmt == "e4m3":
        words = by_word.astype(ml_dtypes.float8_e4m3fn).view(np.uint8)
    else:
        c = by_word.astype(ml_dtypes.float4_e2m1fn).view(np.uint8) & 0xF
        words = (c[..., 0::2] | (c[..., 1::2] << 4)).reshape(k // 512, 128, 2 * n)
    return np.ascontiguousarray(words), np.ascontiguousarray(byte.astype(np.uint8).reshape(k // 512, 16, n))


def unpack_weight(words, scales, fmt):
    g, _, n = scales.shape
    words = np.ascontiguousarray(words).reshape(g, 128, n, -1)
    if fmt == "e4m3":
        vals = words.view(ml_dtypes.float8_e4m3fn).astype(np.float64)
    else:
        nib = np.empty((g, 128, n, 4), np.uint8)
        nib[..., 0::2] = words & 0xF
        nib[..., 1::2] = words >> 4
        vals = E2M1[nib]
    vals = vals * np.repeat(np.exp2(scales.astype(np.float64) - 127.0), 8, axis=1)[..., None]
    return vals.transpose(0, 1, 3, 2).reshape(g * 512, n)


def pack_table(v):
    words, scales = pack_weight(v, "e4m3")
    return np.concatenate([words.reshape(words.shape[0], -1), scales.reshape(scales.shape[0], -1)], axis=1)


def unpack_table(tab):
    g, t = tab.shape[0], tab.shape[1] // 528
    return unpack_weight(tab[:, :512 * t].reshape(g, 128, t, 4), tab[:, 512 * t:].reshape(g, 16, t), "e4m3")


def gelu(v):
    return 0.5 * v * (1.0 + np.tanh(np.sqrt(2.0 / np.pi) * (v + 0.044715 * v**3)))


K, M, T, S = 1536, 128, 4096, 2048


def setup_inputs():
    n = np.random.standard_normal
    s = mx_kscale(K)[:, None]
    u = mx_kscale(512)[:, None]
    p_w2 = pack_weight(1.4 * n((512, M)) / np.sqrt(512) / u, "e2m1")
    return {
        "tab": pack_table(n((K, T)) * s),
        "w1": (n((K, 512)) / np.sqrt(K) / s * u.T).astype(np.float32),
        "w2_words": p_w2[0],
        "w2_scales": p_w2[1],
        "b": (0.3 * n(128)).astype(np.float32),
        "wgo": np.tile(np.random.uniform(0.5, 2.0, S), (128, 1)).astype(np.float32),
        "offs": striped(np.random.permutation(T)[:S]),
        "offs2": striped(np.random.permutation(T)[:S]),
    }


def reference(tab, w1, w2_words, w2_scales, b, wgo, offs, offs2):
    tab_ = unpack_table(tab)[:, unstriped(offs)]
    w1_ = mxq(f64(w1), 0, "e4m3")
    w2_ = unpack_weight(w2_words, w2_scales, "e2m1")
    h_ = mxq(np.maximum(w1_.T @ tab_, 0.0), 0, "e4m3")
    y = w2_.T @ h_
    out = np.zeros((M, T))
    out[:, unstriped(offs2)] = f64(wgo)[0] * (gelu(y + f64(b)[:, None]))
    return out

@@ -1,0 +1,191 @@
+from contextlib import ExitStack
+
+import concourse.mybir as mybir
+
+K, M, T, S, H = 1536, 128, 4096, 2048, 512
+FLOPS = 2 * K * H * S + 2 * H * M * S
+
+F32 = mybir.dt.float32
+BF16 = mybir.dt.bfloat16
+I32 = mybir.dt.int32
+U32 = mybir.dt.uint32
+U16 = mybir.dt.uint16
+U8 = mybir.dt.uint8
+E4M3X4 = mybir.dt.float8_e4m3fn_x4
+E2M1X4 = mybir.dt.float4_e2m1fn_x4
+ACT = mybir.ActivationFunctionType
+
+P = 128
+PACK = 4
+K_PASS = P * PACK
+PASSES = K // K_PASS
+LAST = PASSES - 1
+GROUP = 128
+GROUPS = S // GROUP
+SLICE = 512
+SLICES = S // SLICE
+PER_SLICE = SLICE // GROUP
+H_BANKS = 6
+Y_BANKS = 2
+HALF = S // 2
+
+
+def tile_list_tabscat_m_gelu_kernel(tc, tab, w1, w2_words, w2_scales, b, wgo, offs, offs2, out):
+    nc = tc.nc
+    tab_words = tab.bitcast(I32)
+
+    with ExitStack() as ctx:
+        held = ctx.enter_context(tc.tile_pool(name="held", bufs=1))
+        h_psum = ctx.enter_context(tc.psum_pool(name="h_psum", bufs=H_BANKS))
+        y_psum = ctx.enter_context(tc.psum_pool(name="y_psum", bufs=Y_BANKS))
+
+        def keep(name, shape, dtype, tag=None):
+            return held.tile(shape, dtype, name=name, tag=tag or name, align_bytes=64)
+
+        idx = keep("idx", [P, S // 16], U16)
+        idx2 = keep("idx2", [P, S // 16], U16)
+        cache_words = [keep("cache_words%d" % a, [P, T], I32) for a in range(PASSES)]
+        cache_scales = keep("cache_scales", [P, T], U8)
+        w1_rows = [keep("w1_rows%d" % a, [P, PACK, H], F32) for a in range(PASSES)]
+        w2_codes = keep("w2_codes", [P, 2 * M], U8)
+        w2_plane = keep("w2_plane", [P, M], U8)
+        bias = keep("bias", [P, 1], F32)
+        place_weight = keep("place_weight", [P, S], F32)
+        page = keep("page", [P, T], F32)
+        warm_in = keep("warm_in", [P, 1], F32)
+        warm_out = keep("warm_out", [P, 1], F32)
+
+        nc.vector.memset(cache_scales[:].bitcast(I32), 0)
+        nc.vector.memset(w2_plane[:].bitcast(I32), 0)
+        nc.vector.memset(warm_in[:], 0.0)
+        nc.vector.memset(page[:, : T // 2 - 1], 0.0)
+        nc.vector.memset(page[:, T // 2 - 1 :], 0.0)
+        nc.scalar.activation(warm_out[:], warm_in[:], ACT.Gelu_apprx_tanh)
+
+        def load_words(a):
+            nc.sync.dma_start(cache_words[a][:], tab_words[a, : P * T].rearrange("(p t) -> p t", p=P))
+
+        def load_w1(a):
+            nc.sync.dma_start(w1_rows[a][:], w1[a * K_PASS : (a + 1) * K_PASS, :].rearrange("(p j) c -> p j c", j=PACK))
+
+        nc.sync.dma_start(idx[:], offs)
+        load_words(0)
+        load_w1(0)
+        load_w1(1)
+        load_words(1)
+        load_w1(2)
+        load_words(2)
+        nc.sync.dma_start(idx2[:], offs2)
+        nc.sync.dma_start(place_weight[:], wgo)
+
+        for q in range(4):
+            rows = tab_words[:, P * T + q * T : P * T + (q + 1) * T].rearrange("a (r t) -> a r t", r=4)
+            nc.gpsimd.dma_start(cache_scales[32 * q : 32 * q + 4 * PASSES, :].bitcast(I32), rows)
+        nc.gpsimd.dma_start(w2_codes[:].bitcast(I32), w2_words[0].bitcast(I32))
+        for q in range(4):
+            nc.gpsimd.dma_start(w2_plane[32 * q : 32 * q + 4, :].bitcast(I32), w2_scales[0, 4 * q : 4 * q + 4, :].bitcast(I32))
+        nc.gpsimd.dma_start(bias[:], b.rearrange("(p o) -> p o", o=1))
+
+        def gather(dst, window, first, count):
+            nc.vector.tensor_copy(dst, window.indirect(idx[:, first // 16 : (first + count) // 16]))
+
+        picked_scales = keep("picked_scales", [P, S], U8)
+        picked = {}
+
+        def gather_words(a, first, count, tag=None):
+            tile_ = keep("picked%d_%d" % (a, first), [P, count], U32, tag)
+            gather(tile_[:], cache_words[a][:].bitcast(U32), first, count)
+            for g in range(first // GROUP, (first + count) // GROUP):
+                picked[a, g] = tile_[:, g * GROUP - first : (g + 1) * GROUP - first]
+
+        w1_codes, w1_planes = {}, {}
+
+        def quantise_w1(a):
+            rounded = keep("w1_rounded%d" % a, [P, PACK * H], BF16)
+            nc.scalar.copy(
+                rounded[:].rearrange("p (t m j) -> p m j t", t=PACK, j=PACK),
+                w1_rows[a][:].rearrange("p j (m t) -> p m j t", t=PACK),
+            )
+            w1_codes[a] = keep("w1_codes%d" % a, [P, H], U32)
+            w1_planes[a] = keep("w1_plane%d" % a, [P, H], U8)
+            nc.vector.quantize_mx(w1_codes[a][:].bitcast(E4M3X4), w1_planes[a][:], rounded[:])
+
+        for first in (0, HALF):
+            gather(picked_scales[:, first : first + HALF], cache_scales[:], first, HALF)
+        for a in range(LAST):
+            for first in (0, HALF):
+                gather_words(a, first, HALF)
+            quantise_w1(a)
+        quantise_w1(LAST)
+
+        banks = {}
+
+        def first_layer_pass(g, a):
+            if a == 0:
+                banks[g] = h_psum.tile([P, PACK, GROUP], F32, name="h_bank")
+            for t in range(PACK):
+                nc.tensor.matmul_mx(
+                    banks[g][:, t, :],
+                    lhsT=w1_codes[a][:, t * P : (t + 1) * P].bitcast(E4M3X4),
+                    lhsT_scale=w1_planes[a][:, t * P : (t + 1) * P],
+                    rhs=picked[a, g].bitcast(E4M3X4),
+                    rhs_scale=picked_scales[4 * a :, g * GROUP : (g + 1) * GROUP],
+                    start=(a == 0 and t == 0),
+                    stop=(a == LAST and t == PACK - 1),
+                )
+
+        for a in range(LAST):
+            for g in range(H_BANKS):
+                first_layer_pass(g, a)
+
+        for s in range(SLICES - 1):
+            gather_words(LAST, s * SLICE, SLICE)
+
+        h_codes, h_planes = {}, {}
+
+        def hidden(g):
+            for a in range(LAST if g < H_BANKS else 0, PASSES):
+                first_layer_pass(g, a)
+            h = keep("h%d" % g, [P, GROUP * PACK], BF16)
+            nc.scalar.activation(
+                h[:].rearrange("p (n t) -> p n t", t=PACK), banks[g][:].rearrange("p t n -> p n t"), ACT.Relu
+            )
+            h_codes[g] = keep("h_codes%d" % g, [P, GROUP], U32)
+            h_planes[g] = keep("h_plane%d" % g, [P, GROUP], U8)
+            nc.vector.quantize_mx(h_codes[g][:].bitcast(E4M3X4), h_planes[g][:], h[:])
+            if g == PER_SLICE - 1:
+                gather_words(LAST, S - SLICE, SLICE, tag="h%d" % g)
+
+        results = [keep("result%d" % s, [P, SLICE], F32) for s in range(SLICES)]
+
+        def second_layer(g):
+            y = y_psum.tile([M, GROUP], F32, name="y")
+            nc.tensor.matmul_mx(
+                y[:],
+                lhsT=w2_codes[:].bitcast(E2M1X4),
+                lhsT_scale=w2_plane[:],
+                rhs=h_codes[g][:].bitcast(E4M3X4),
+                rhs_scale=h_planes[g][:],
+                start=True,
+                stop=True,
+            )
+            s, r = divmod(g, PER_SLICE)
+            nc.scalar.activation(results[s][:, r * GROUP : (r + 1) * GROUP], y[:], ACT.Gelu_apprx_tanh, bias=bias[:])
+
+        done = 0
+        for s in range(SLICES):
+            ahead = PER_SLICE + 1 if s == 0 else min(GROUPS, (s + 2) * PER_SLICE)
+            for g in range(done, ahead):
+                hidden(g)
+            done = ahead
+            for g in range(s * PER_SLICE, (s + 1) * PER_SLICE):
+                second_layer(g)
+            nc.vector.tensor_tensor(
+                page[:].indirect(idx2[:, s * SLICE // 16 : (s + 1) * SLICE // 16]),
+                results[s][:],
+                place_weight[:, s * SLICE : (s + 1) * SLICE],
+                mybir.AluOpType.mult,
+            )
+
+        nc.sync.dma_start(out[:, : T // 2], page[:, : T // 2])
+        nc.scalar.dma_start(out[:, T // 2 :], page[:, T // 2 :])

@@ -25,8 +25,7 @@ GROUPS = S // GROUP
 SLICE = 512
 SLICES = S // SLICE
 PER_SLICE = SLICE // GROUP
-H_BANKS = 6
-Y_BANKS = 2
+BANKS = 8
 HALF = S // 2
 
 
@@ -36,8 +35,7 @@ def tile_list_tabscat_m_gelu_kernel(tc, tab, w1, w2_words, w2_scales, b, wgo, of
 
     with ExitStack() as ctx:
         held = ctx.enter_context(tc.tile_pool(name="held", bufs=1))
-        h_psum = ctx.enter_context(tc.psum_pool(name="h_psum", bufs=H_BANKS))
-        y_psum = ctx.enter_context(tc.psum_pool(name="y_psum", bufs=Y_BANKS))
+        psum = ctx.enter_context(tc.psum_pool(name="psum", bufs=1))
 
         def keep(name, shape, dtype, tag=None):
             return held.tile(shape, dtype, name=name, tag=tag or name, align_bytes=64)
@@ -68,28 +66,29 @@ def tile_list_tabscat_m_gelu_kernel(tc, tab, w1, w2_words, w2_scales, b, wgo, of
         def load_w1(a):
             nc.sync.dma_start(w1_rows[a][:], w1[a * K_PASS : (a + 1) * K_PASS, :].rearrange("(p j) c -> p j c", j=PACK))
 
+        def load_scale_rows():
+            for q in range(4):
+                rows = tab_words[:, P * T + q * T : P * T + (q + 1) * T].rearrange("a (r t) -> a r t", r=4)
+                nc.gpsimd.dma_start(cache_scales[32 * q : 32 * q + 4 * PASSES, :].bitcast(I32), rows)
+
         nc.sync.dma_start(idx[:], offs)
         load_words(0)
+        load_scale_rows()
         load_w1(0)
         load_w1(1)
         load_words(1)
         load_w1(2)
         load_words(2)
+        nc.sync.dma_start(w2_codes[:].bitcast(I32), w2_words[0].bitcast(I32))
+        for q in range(4):
+            nc.sync.dma_start(w2_plane[32 * q : 32 * q + 4, :].bitcast(I32), w2_scales[0, 4 * q : 4 * q + 4, :].bitcast(I32))
+        nc.sync.dma_start(bias[:], b.rearrange("(p o) -> p o", o=1))
         nc.sync.dma_start(idx2[:], offs2)
         nc.sync.dma_start(place_weight[:], wgo)
-
-        for q in range(4):
-            rows = tab_words[:, P * T + q * T : P * T + (q + 1) * T].rearrange("a (r t) -> a r t", r=4)
-            nc.gpsimd.dma_start(cache_scales[32 * q : 32 * q + 4 * PASSES, :].bitcast(I32), rows)
-        nc.gpsimd.dma_start(w2_codes[:].bitcast(I32), w2_words[0].bitcast(I32))
-        for q in range(4):
-            nc.gpsimd.dma_start(w2_plane[32 * q : 32 * q + 4, :].bitcast(I32), w2_scales[0, 4 * q : 4 * q + 4, :].bitcast(I32))
-        nc.gpsimd.dma_start(bias[:], b.rearrange("(p o) -> p o", o=1))
 
         def gather(dst, window, first, count):
             nc.vector.tensor_copy(dst, window.indirect(idx[:, first // 16 : (first + count) // 16]))
 
-        picked_scales = keep("picked_scales", [P, S], U8)
         picked = {}
 
         def gather_words(a, first, count, tag=None):
@@ -110,19 +109,20 @@ def tile_list_tabscat_m_gelu_kernel(tc, tab, w1, w2_words, w2_scales, b, wgo, of
             w1_planes[a] = keep("w1_plane%d" % a, [P, H], U8)
             nc.vector.quantize_mx(w1_codes[a][:].bitcast(E4M3X4), w1_planes[a][:], rounded[:])
 
+        gather_words(0, 0, S)
+        picked_scales = keep("picked_scales", [P, S], U8, tag="cache_words0")
+        gather(picked_scales[:], cache_scales[:], 0, S)
+        quantise_w1(0)
+        quantise_w1(1)
         for first in (0, HALF):
-            gather(picked_scales[:, first : first + HALF], cache_scales[:], first, HALF)
-        for a in range(LAST):
-            for first in (0, HALF):
-                gather_words(a, first, HALF)
-            quantise_w1(a)
+            gather_words(1, first, HALF)
         quantise_w1(LAST)
 
         banks = {}
 
         def first_layer_pass(g, a):
             if a == 0:
-                banks[g] = h_psum.tile([P, PACK, GROUP], F32, name="h_bank")
+                banks[g] = psum.tile([P, PACK, GROUP], F32, name="h_bank%d" % g, tag="bank%d" % (g if g < BANKS else PER_SLICE + g % PER_SLICE))
             for t in range(PACK):
                 nc.tensor.matmul_mx(
                     banks[g][:, t, :],
@@ -135,51 +135,60 @@ def tile_list_tabscat_m_gelu_kernel(tc, tab, w1, w2_words, w2_scales, b, wgo, of
                 )
 
         for a in range(LAST):
-            for g in range(H_BANKS):
+            for g in range(BANKS):
                 first_layer_pass(g, a)
 
         for s in range(SLICES - 1):
             gather_words(LAST, s * SLICE, SLICE)
 
-        h_codes, h_planes = {}, {}
+        runs = [(g, 1) for g in range(BANKS)] + [(g, PER_SLICE) for g in range(BANKS, GROUPS, PER_SLICE)]
+        run_of = {g: run for run in runs for g in range(run[0], run[0] + run[1])}
+        h_rounded, h_codes, h_planes = {}, {}, {}
 
         def hidden(g):
-            for a in range(LAST if g < H_BANKS else 0, PASSES):
+            for a in range(LAST if g < BANKS else 0, PASSES):
                 first_layer_pass(g, a)
-            h = keep("h%d" % g, [P, GROUP * PACK], BF16)
+            first, count = run_of[g]
+            if g == first:
+                h_rounded[first] = keep("h%d" % first, [P, count * GROUP * PACK], BF16)
+            h = h_rounded[first][:, (g - first) * GROUP * PACK : (g - first + 1) * GROUP * PACK]
             nc.scalar.activation(
-                h[:].rearrange("p (n t) -> p n t", t=PACK), banks[g][:].rearrange("p t n -> p n t"), ACT.Relu
+                h.rearrange("p (n t) -> p n t", t=PACK), banks[g][:].rearrange("p t n -> p n t"), ACT.Relu
             )
-            h_codes[g] = keep("h_codes%d" % g, [P, GROUP], U32)
-            h_planes[g] = keep("h_plane%d" % g, [P, GROUP], U8)
-            nc.vector.quantize_mx(h_codes[g][:].bitcast(E4M3X4), h_planes[g][:], h[:])
+            if g == first + count - 1:
+                h_codes[first] = keep("h_codes%d" % first, [P, count * GROUP], U32)
+                h_planes[first] = keep("h_plane%d" % first, [P, count * GROUP], U8)
+                nc.vector.quantize_mx(h_codes[first][:].bitcast(E4M3X4), h_planes[first][:], h_rounded[first][:])
             if g == PER_SLICE - 1:
                 gather_words(LAST, S - SLICE, SLICE, tag="h%d" % g)
 
         results = [keep("result%d" % s, [P, SLICE], F32) for s in range(SLICES)]
 
-        def second_layer(g):
-            y = y_psum.tile([M, GROUP], F32, name="y")
+        def second_layer(first, count):
+            s, r = divmod(first, PER_SLICE)
+            y = psum.tile([M, count * GROUP], F32, name="y%d" % first, tag="bank%d" % (r if count == 1 else s % 2))
             nc.tensor.matmul_mx(
                 y[:],
                 lhsT=w2_codes[:].bitcast(E2M1X4),
                 lhsT_scale=w2_plane[:],
-                rhs=h_codes[g][:].bitcast(E4M3X4),
-                rhs_scale=h_planes[g][:],
+                rhs=h_codes[first][:].bitcast(E4M3X4),
+                rhs_scale=h_planes[first][:],
                 start=True,
                 stop=True,
             )
-            s, r = divmod(g, PER_SLICE)
-            nc.scalar.activation(results[s][:, r * GROUP : (r + 1) * GROUP], y[:], ACT.Gelu_apprx_tanh, bias=bias[:])
+            nc.scalar.activation(
+                results[s][:, r * GROUP : (r + count) * GROUP], y[:], ACT.Gelu_apprx_tanh, bias=bias[:]
+            )
 
         done = 0
         for s in range(SLICES):
-            ahead = PER_SLICE + 1 if s == 0 else min(GROUPS, (s + 2) * PER_SLICE)
+            ahead = min(GROUPS, (2 * s + 1) * PER_SLICE + 1)
             for g in range(done, ahead):
                 hidden(g)
             done = ahead
-            for g in range(s * PER_SLICE, (s + 1) * PER_SLICE):
-                second_layer(g)
+            for first, count in runs:
+                if first // PER_SLICE == s:
+                    second_layer(first, count)
             nc.vector.tensor_tensor(
                 page[:].indirect(idx2[:, s * SLICE // 16 : (s + 1) * SLICE // 16]),
                 results[s][:],

from contextlib import ExitStack

import concourse.mybir as mybir

K, M, T, S, H = 1536, 128, 4096, 2048, 512
FLOPS = 2 * K * H * S + 2 * H * M * S

F32 = mybir.dt.float32
BF16 = mybir.dt.bfloat16
I32 = mybir.dt.int32
U32 = mybir.dt.uint32
U16 = mybir.dt.uint16
U8 = mybir.dt.uint8
E4M3X4 = mybir.dt.float8_e4m3fn_x4
E2M1X4 = mybir.dt.float4_e2m1fn_x4
ACT = mybir.ActivationFunctionType

P = 128
PACK = 4
K_PASS = P * PACK
PASSES = K // K_PASS
LAST = PASSES - 1
GROUP = 128
GROUPS = S // GROUP
SLICE = 512
SLICES = S // SLICE
PER_SLICE = SLICE // GROUP
BANKS = 8
HALF = S // 2


def tile_list_tabscat_m_gelu_kernel(tc, tab, w1, w2_words, w2_scales, b, wgo, offs, offs2, out):
    nc = tc.nc
    tab_words = tab.bitcast(I32)

    with ExitStack() as ctx:
        held = ctx.enter_context(tc.tile_pool(name="held", bufs=1))
        psum = ctx.enter_context(tc.psum_pool(name="psum", bufs=1))

        def keep(name, shape, dtype, tag=None):
            return held.tile(shape, dtype, name=name, tag=tag or name, align_bytes=64)

        idx = keep("idx", [P, S // 16], U16)
        idx2 = keep("idx2", [P, S // 16], U16)
        cache_words = [keep("cache_words%d" % a, [P, T], I32) for a in range(PASSES)]
        cache_scales = keep("cache_scales", [P, T], U8)
        w1_rows = [keep("w1_rows%d" % a, [P, PACK, H], F32) for a in range(PASSES)]
        w2_codes = keep("w2_codes", [P, 2 * M], U8)
        w2_plane = keep("w2_plane", [P, M], U8)
        bias = keep("bias", [P, 1], F32)
        place_weight = keep("place_weight", [P, S], F32)
        page = keep("page", [P, T], F32)
        warm_in = keep("warm_in", [P, 1], F32)
        warm_out = keep("warm_out", [P, 1], F32)

        nc.vector.memset(cache_scales[:].bitcast(I32), 0)
        nc.vector.memset(w2_plane[:].bitcast(I32), 0)
        nc.vector.memset(warm_in[:], 0.0)
        nc.vector.memset(page[:, : T // 2 - 1], 0.0)
        nc.vector.memset(page[:, T // 2 - 1 :], 0.0)
        nc.scalar.activation(warm_out[:], warm_in[:], ACT.Gelu_apprx_tanh)

        def load_words(a):
            nc.sync.dma_start(cache_words[a][:], tab_words[a, : P * T].rearrange("(p t) -> p t", p=P))

        def load_w1(a):
            nc.sync.dma_start(w1_rows[a][:], w1[a * K_PASS : (a + 1) * K_PASS, :].rearrange("(p j) c -> p j c", j=PACK))

        def load_scale_rows():
            for q in range(4):
                rows = tab_words[:, P * T + q * T : P * T + (q + 1) * T].rearrange("a (r t) -> a r t", r=4)
                nc.gpsimd.dma_start(cache_scales[32 * q : 32 * q + 4 * PASSES, :].bitcast(I32), rows)

        nc.sync.dma_start(idx[:], offs)
        load_words(0)
        load_scale_rows()
        load_w1(0)
        load_w1(1)
        load_words(1)
        load_w1(2)
        load_words(2)
        nc.sync.dma_start(w2_codes[:].bitcast(I32), w2_words[0].bitcast(I32))
        for q in range(4):
            nc.sync.dma_start(w2_plane[32 * q : 32 * q + 4, :].bitcast(I32), w2_scales[0, 4 * q : 4 * q + 4, :].bitcast(I32))
        nc.sync.dma_start(bias[:], b.rearrange("(p o) -> p o", o=1))
        nc.sync.dma_start(idx2[:], offs2)
        nc.sync.dma_start(place_weight[:], wgo)

        def gather(dst, window, first, count):
            nc.vector.tensor_copy(dst, window.indirect(idx[:, first // 16 : (first + count) // 16]))

        picked = {}

        def gather_words(a, first, count, tag=None):
            tile_ = keep("picked%d_%d" % (a, first), [P, count], U32, tag)
            gather(tile_[:], cache_words[a][:].bitcast(U32), first, count)
            for g in range(first // GROUP, (first + count) // GROUP):
                picked[a, g] = tile_[:, g * GROUP - first : (g + 1) * GROUP - first]

        w1_codes, w1_planes = {}, {}

        def quantise_w1(a):
            rounded = keep("w1_rounded%d" % a, [P, PACK * H], BF16)
            nc.scalar.copy(
                rounded[:].rearrange("p (t m j) -> p m j t", t=PACK, j=PACK),
                w1_rows[a][:].rearrange("p j (m t) -> p m j t", t=PACK),
            )
            w1_codes[a] = keep("w1_codes%d" % a, [P, H], U32)
            w1_planes[a] = keep("w1_plane%d" % a, [P, H], U8)
            nc.vector.quantize_mx(w1_codes[a][:].bitcast(E4M3X4), w1_planes[a][:], rounded[:])

        gather_words(0, 0, S)
        picked_scales = keep("picked_scales", [P, S], U8, tag="cache_words0")
        gather(picked_scales[:], cache_scales[:], 0, S)
        quantise_w1(0)
        quantise_w1(1)
        for first in (0, HALF):
            gather_words(1, first, HALF)
        quantise_w1(LAST)

        banks = {}

        def first_layer_pass(g, a):
            if a == 0:
                banks[g] = psum.tile([P, PACK, GROUP], F32, name="h_bank%d" % g, tag="bank%d" % (g if g < BANKS else PER_SLICE + g % PER_SLICE))
            for t in range(PACK):
                nc.tensor.matmul_mx(
                    banks[g][:, t, :],
                    lhsT=w1_codes[a][:, t * P : (t + 1) * P].bitcast(E4M3X4),
                    lhsT_scale=w1_planes[a][:, t * P : (t + 1) * P],
                    rhs=picked[a, g].bitcast(E4M3X4),
                    rhs_scale=picked_scales[4 * a :, g * GROUP : (g + 1) * GROUP],
                    start=(a == 0 and t == 0),
                    stop=(a == LAST and t == PACK - 1),
                )

        for a in range(LAST):
            for g in range(BANKS):
                first_layer_pass(g, a)

        for s in range(SLICES - 1):
            gather_words(LAST, s * SLICE, SLICE)

        runs = [(g, 1) for g in range(BANKS)] + [(g, PER_SLICE) for g in range(BANKS, GROUPS, PER_SLICE)]
        run_of = {g: run for run in runs for g in range(run[0], run[0] + run[1])}
        h_rounded, h_codes, h_planes = {}, {}, {}

        def hidden(g):
            for a in range(LAST if g < BANKS else 0, PASSES):
                first_layer_pass(g, a)
            first, count = run_of[g]
            if g == first:
                h_rounded[first] = keep("h%d" % first, [P, count * GROUP * PACK], BF16)
            h = h_rounded[first][:, (g - first) * GROUP * PACK : (g - first + 1) * GROUP * PACK]
            nc.scalar.activation(
                h.rearrange("p (n t) -> p n t", t=PACK), banks[g][:].rearrange("p t n -> p n t"), ACT.Relu
            )
            if g == first + count - 1:
                h_codes[first] = keep("h_codes%d" % first, [P, count * GROUP], U32)
                h_planes[first] = keep("h_plane%d" % first, [P, count * GROUP], U8)
                nc.vector.quantize_mx(h_codes[first][:].bitcast(E4M3X4), h_planes[first][:], h_rounded[first][:])
            if g == PER_SLICE - 1:
                gather_words(LAST, S - SLICE, SLICE, tag="h%d" % g)

        results = [keep("result%d" % s, [P, SLICE], F32) for s in range(SLICES)]

        def second_layer(first, count):
            s, r = divmod(first, PER_SLICE)
            y = psum.tile([M, count * GROUP], F32, name="y%d" % first, tag="bank%d" % (r if count == 1 else s % 2))
            nc.tensor.matmul_mx(
                y[:],
                lhsT=w2_codes[:].bitcast(E2M1X4),
                lhsT_scale=w2_plane[:],
                rhs=h_codes[first][:].bitcast(E4M3X4),
                rhs_scale=h_planes[first][:],
                start=True,
                stop=True,
            )
            nc.scalar.activation(
                results[s][:, r * GROUP : (r + count) * GROUP], y[:], ACT.Gelu_apprx_tanh, bias=bias[:]
            )

        done = 0
        for s in range(SLICES):
            ahead = min(GROUPS, (2 * s + 1) * PER_SLICE + 1)
            for g in range(done, ahead):
                hidden(g)
            done = ahead
            for first, count in runs:
                if first // PER_SLICE == s:
                    second_layer(first, count)
            nc.vector.tensor_tensor(
                page[:].indirect(idx2[:, s * SLICE // 16 : (s + 1) * SLICE // 16]),
                results[s][:],
                place_weight[:, s * SLICE : (s + 1) * SLICE],
                mybir.AluOpType.mult,
            )

        nc.sync.dma_start(out[:, : T // 2], page[:, : T // 2])
        nc.scalar.dma_start(out[:, T // 2 :], page[:, T // 2 :])
